import numpy as np
import ml_dtypes


def mxq(x, axis, fmt="e4m3"):
    dtype, down = {"e4m3": (ml_dtypes.float8_e4m3fn, 7), "e5m2": (ml_dtypes.float8_e5m2, 14)}[fmt]
    v = np.moveaxis(np.asarray(x, np.float32).astype(ml_dtypes.bfloat16).astype(np.float64), axis, -1)
    blocks = v.reshape(v.shape[:-1] + (-1, 32))
    amax = np.abs(blocks).max(-1, keepdims=True)
    byte = np.maximum(np.where(amax > 0, np.frexp(amax)[1] - 1 + 127, 0) - down, 1)
    scale = np.exp2(byte - 127.0)
    codes = (blocks / scale).astype(np.float32).astype(dtype).astype(np.float64)
    return np.moveaxis((codes * scale).reshape(v.shape), -1, axis)


WIDE = False


def mx_kscale(k):
    if not WIDE:
        return np.ones(k)
    levels = np.array([10, -10, 5, -5, 0])
    if k % 512:
        return np.exp2(np.random.permutation(np.resize(levels, k // 32))).repeat(32)
    a = np.empty((k // 512, 16))
    for p in range(k // 512):
        a[p, :8] = np.random.permutation(np.resize(levels, 8))
        for g in range(8):
            far = levels[np.abs(levels - a[p, g]) >= 10]
            a[p, g + 8] = far[np.random.randint(len(far))]
    return np.exp2(a.ravel()).repeat(32)


def f64(x):
    return np.asarray(x).astype(np.float64)


def striped8(idx):
    return np.asarray(idx).reshape(8, -1, 16).transpose(0, 2, 1).reshape(128, -1).astype(np.uint16)


def unstriped8(offs):
    return offs.reshape(8, 16, -1).transpose(0, 2, 1).reshape(8, -1).astype(np.int64)


def pick8(x, idx, run):
    r = np.arange(len(x))
    return x[r[:, None], idx[r % (8 * run) // run]]


E2M1 = np.array([0.0, 0.5, 1.0, 1.5, 2.0, 3.0, 4.0, 6.0, -0.0, -0.5, -1.0, -1.5, -2.0, -3.0, -4.0, -6.0])


def pack_weight(w, fmt):
    k, n = w.shape
    w = f64(np.asarray(w, np.float32).astype(ml_dtypes.bfloat16)).reshape(k // 32, 32, n)
    amax = np.abs(w).max(1)
    if fmt == "e4m3":
        byte = np.frexp(amax)[1] - 1 + 127 - 7
    else:
        mant, ex = np.frexp(amax / 6.0)
        byte = np.where(mant > 0.5, ex, ex - 1) + 127
    byte = np.clip(np.where(amax > 0, byte, 1), 1, 254)
    scaled = (w * np.exp2(127.0 - byte)[:, None, :]).reshape(k, n).astype(np.float32)
    by_word = np.ascontiguousarray(scaled.reshape(k // 512, 128, 4, n).transpose(0, 1, 3, 2))
    if fmt == "e4m3":
        words = by_word.astype(ml_dtypes.float8_e4m3fn).view(np.uint8)
    else:
        c = by_word.astype(ml_dtypes.float4_e2m1fn).view(np.uint8) & 0xF
        words = (c[..., 0::2] | (c[..., 1::2] << 4)).reshape(k // 512, 128, 2 * n)
    return np.ascontiguousarray(words), np.ascontiguousarray(byte.astype(np.uint8).reshape(k // 512, 16, n))


def unpack_weight(words, scales, fmt):
    g, _, n = scales.shape
    words = np.ascontiguousarray(words).reshape(g, 128, n, -1)
    if fmt == "e4m3":
        vals = words.view(ml_dtypes.float8_e4m3fn).astype(np.float64)
    else:
        nib = np.empty((g, 128, n, 4), np.uint8)
        nib[..., 0::2] = words & 0xF
        nib[..., 1::2] = words >> 4
        vals = E2M1[nib]
    vals = vals * np.repeat(np.exp2(scales.astype(np.float64) - 127.0), 8, axis=1)[..., None]
    return vals.transpose(0, 1, 3, 2).reshape(g * 512, n)


D, T, U, I, Q = 512, 1024, 1024, 512, 128


def setup_inputs():
    n = np.random.standard_normal
    idx = np.stack([np.random.permutation(T)[:I] for _ in range(8)])
    idx2 = np.stack([np.random.permutation(U)[:I] for _ in range(8)])
    idx3 = np.stack([np.random.permutation(T)[:I] for _ in range(8)])
    idx4 = np.stack([np.random.permutation(U)[:I] for _ in range(8)])
    idx5 = np.stack([np.random.permutation(U)[:I] for _ in range(8)])
    fd = mx_kscale(D)
    keysp = pack_weight(n((D, T)) / fd[:, None], "e2m1")
    notesp = pack_weight(n((D, U)) / fd[:, None], "e4m3")
    return {
        "query": (n((D, Q)) * 1.0 / np.sqrt(D) * fd[:, None]).astype(np.float32),
        "keys_words": keysp[0],
        "keys_scales": keysp[1],
        "notes_words": notesp[0],
        "notes_scales": notesp[1],
        "offs": striped8(idx),
        "offs2": striped8(idx2),
        "offs3": striped8(idx3),
        "offs4": striped8(idx4),
        "offs5": striped8(idx5),
    }


def reference(query, keys_words, keys_scales, notes_words, notes_scales, offs, offs2, offs3, offs4, offs5):
    idx = unstriped8(offs)
    idx2 = unstriped8(offs2)
    idx3 = unstriped8(offs3)
    idx4 = unstriped8(offs4)
    idx5 = unstriped8(offs5)
    keysu = unpack_weight(keys_words, keys_scales, "e2m1")
    notesu = unpack_weight(notes_words, notes_scales, "e4m3")
    queryq = mxq(f64(query), 0, "e4m3")
    a = queryq.T @ keysu
    b = queryq.T @ notesu
    lo1 = np.minimum(pick8(a, idx, 16), pick8(b, idx2, 16))
    hi1 = np.maximum(pick8(a, idx3, 16), pick8(b, idx2, 16))
    r = hi1 - lo1
    f1 = np.zeros((Q, U))
    f1[np.arange(Q)[:, None], idx4[np.arange(Q) % 128 // 16]] = r
    bb = b - f1
    y = pick8(bb, idx5, 16) + lo1
    return y

@@ -1,0 +1,132 @@
+from contextlib import ExitStack
+
+import concourse.mybir as mybir
+
+D, T, U, SLOTS, Q = 512, 1024, 1024, 512, 128
+FLOPS = 2 * D * Q * (T + U)
+
+F32 = mybir.dt.float32
+BF16 = mybir.dt.bfloat16
+I32 = mybir.dt.int32
+U32 = mybir.dt.uint32
+U16 = mybir.dt.uint16
+U8 = mybir.dt.uint8
+FP8X4 = mybir.dt.float8_e4m3fn_x4
+FP4X4 = mybir.dt.float4_e2m1fn_x4
+ALU = mybir.AluOpType
+COPY = mybir.ActivationFunctionType.Copy
+
+P = 128
+PACK = 4
+HALF = SLOTS // 2
+HALF_COLS = HALF // 16
+
+
+def tile_attend_clippedgap_two_kernel(tc, query, keys_words, keys_scales, notes_words, notes_scales,
+                                       offs, offs2, offs3, offs4, offs5, out):
+    nc = tc.nc
+    with ExitStack() as ctx:
+        sb = ctx.enter_context(tc.tile_pool(name="sb", bufs=1))
+        ps = ctx.enter_context(tc.psum_pool(name="ps", bufs=1))
+
+        lists = [sb.tile([P, SLOTS // 16], U16, name="list%d" % n) for n in range(5)]
+        l_a1, l_b2, l_a3, l_put, l_bb = lists
+
+        key_scale = sb.tile([P, T], U8, align_bytes=64)
+        note_scale = sb.tile([P, U], U8, align_bytes=64)
+        gaps = sb.tile([P, U], F32)
+        nc.vector.memset(gaps[:], 0.0)
+
+        def load_scales(plane, rows):
+            for quad in range(4):
+                nc.sync.dma_start(out=plane[32 * quad : 32 * quad + 4, :].bitcast(I32),
+                                  in_=rows[0, 4 * quad : 4 * quad + 4, :].bitcast(I32))
+
+        q_raw = sb.tile([P, PACK, Q], F32)
+        key_words = sb.tile([P, 2 * T], U8, align_bytes=64)
+        note_words = sb.tile([P, U], U32, align_bytes=64, tag="notes_then_third")
+        nc.sync.dma_start(out=q_raw[:], in_=query.rearrange("(p j) q -> p j q", j=PACK))
+        load_scales(key_scale, keys_scales)
+        nc.sync.dma_start(out=key_words[:].bitcast(I32), in_=keys_words[0].bitcast(I32))
+        nc.sync.dma_start(out=note_words[:].bitcast(I32),
+                          in_=notes_words[0].rearrange("p u t -> p (u t)").bitcast(I32))
+        load_scales(note_scale, notes_scales)
+        nc.sync.dma_start(l_a1[:], offs)
+        nc.sync.dma_start(l_a3[:], offs3)
+        nc.sync.dma_start(l_b2[:], offs2)
+        nc.sync.dma_start(l_put[:], offs4)
+        nc.sync.dma_start(l_bb[:], offs5)
+
+        q_bf = sb.tile([P, Q, PACK], BF16, align_bytes=64)
+        nc.vector.tensor_copy(out=q_bf[:], in_=q_raw[:].rearrange("p j q -> p q j"))
+        q_words = sb.tile([P, Q], U32, align_bytes=64)
+        q_scale = sb.tile([P, Q], U8, align_bytes=64)
+        nc.vector.quantize_mx(out=q_words[:].bitcast(FP8X4), scales=q_scale[:],
+                              in_=q_bf[:].rearrange("p q j -> p (q j)"))
+
+        def score(name, rhs, rhs_scale, width):
+            bank = ps.tile([P, width], F32, name=name)
+            nc.tensor.matmul_mx(out=bank[:], lhsT=q_words[:].bitcast(FP8X4), lhsT_scale=q_scale[:],
+                                rhs=rhs, rhs_scale=rhs_scale, start=True, stop=True)
+            return bank
+
+        def key_score(c0, width):
+            return score("a%d" % c0, key_words[:, 2 * c0 : 2 * (c0 + width)].bitcast(FP4X4),
+                         key_scale[:, c0 : c0 + width], width)
+
+        def note_score(c0, width):
+            return score("b%d" % c0, note_words[:, c0 : c0 + width].bitcast(FP8X4),
+                         note_scale[:, c0 : c0 + width], width)
+
+        a = sb.tile([P, T], F32)
+        b = sb.tile([P, U], F32)
+
+        def half(lst, h):
+            return lst[:, h * HALF_COLS : (h + 1) * HALF_COLS]
+
+        a_banks = [(c0, w, key_score(c0, w)) for c0, w in ((0, 512), (512, 256), (768, 256))]
+        b_banks = [(c0, 256, note_score(c0, 256)) for c0 in range(0, U, 256)]
+
+        for n, (c0, w, bank) in enumerate(a_banks):
+            if n == 0:
+                nc.scalar.activation(a[:, c0 : c0 + w], bank[:], COPY)
+            else:
+                nc.vector.tensor_copy(a[:, c0 : c0 + w], bank[:])
+        first = sb.tile([P, HALF], F32, name="first0", tag="first")
+        nc.vector.tensor_copy(first[:], a[:].indirect(half(l_a1, 0)))
+        for n, (c0, w, bank) in enumerate(b_banks):
+            if n < 3:
+                nc.scalar.activation(b[:, c0 : c0 + w], bank[:], COPY)
+            else:
+                nc.vector.tensor_copy(b[:, c0 : c0 + w], bank[:])
+        neg_note = [sb.tile([P, HALF], F32, name="neg_note%d" % h) for h in range(2)]
+        for h in range(2):
+            nc.scalar.activation(neg_note[h][:], b[:].indirect(half(l_b2, h)), COPY, scale=-1.0)
+        third = sb.tile([P, HALF], F32, name="third0", align_bytes=64, tag="notes_then_third")
+        nc.vector.tensor_copy(third[:], a[:].indirect(half(l_a3, 0)))
+
+        neg_lo = [sb.tile([P, HALF], F32, name="neg_lo%d" % h) for h in range(2)]
+        hi = [sb.tile([P, HALF], F32, name="hi%d" % h) for h in range(2)]
+        for h in range(2):
+            if h == 1:
+                first = sb.tile([P, HALF], F32, name="first1", tag="first")
+                nc.scalar.activation(first[:], a[:].indirect(half(l_a1, 1)), COPY)
+                third = sb.tile([P, HALF], F32, name="third1", align_bytes=64, tag="notes_then_third")
+                nc.scalar.activation(third[:], a[:].indirect(half(l_a3, 1)), COPY)
+            nc.vector.scalar_tensor_tensor(out=neg_lo[h][:], in0=first[:], scalar=-1.0, in1=neg_note[h][:],
+                                           op0=ALU.mult, op1=ALU.max)
+            nc.vector.scalar_tensor_tensor(out=hi[h][:], in0=neg_note[h][:], scalar=-1.0, in1=third[:],
+                                           op0=ALU.mult, op1=ALU.max)
+            nc.vector.tensor_tensor(gaps[:].indirect(half(l_put, h)), hi[h][:], neg_lo[h][:], ALU.add)
+
+        bb = sb.tile([P, U], F32)
+        nc.vector.tensor_tensor(bb[:], b[:], gaps[:], ALU.subtract)
+
+        res0 = sb.tile([P, HALF], F32)
+        nc.vector.tensor_tensor(res0[:], bb[:].indirect(half(l_bb, 0)), neg_lo[0][:], ALU.subtract)
+        nc.sync.dma_start(out=out[:, 0:HALF], in_=res0[:])
+        left1 = sb.tile([P, HALF], F32)
+        nc.scalar.activation(left1[:], bb[:].indirect(half(l_bb, 1)), COPY)
+        res1 = sb.tile([P, HALF], F32)
+        nc.vector.tensor_tensor(res1[:], left1[:], neg_lo[1][:], ALU.subtract)
+        nc.scalar.dma_start(out=out[:, HALF:SLOTS], in_=res1[:])

@@ -20,6 +20,8 @@ P = 128
 PACK = 4
 HALF = SLOTS // 2
 HALF_COLS = HALF // 16
+Q_VECTOR = 88
+BB_VECTOR = 768
 
 
 def tile_attend_clippedgap_two_kernel(tc, query, keys_words, keys_scales, notes_words, notes_scales,
@@ -34,35 +36,39 @@ def tile_attend_clippedgap_two_kernel(tc, query, keys_words, keys_scales, notes_
 
         key_scale = sb.tile([P, T], U8, align_bytes=64)
         note_scale = sb.tile([P, U], U8, align_bytes=64)
-        gaps = sb.tile([P, U], F32)
-        nc.vector.memset(gaps[:], 0.0)
 
-        def load_scales(plane, rows):
-            for quad in range(4):
-                nc.sync.dma_start(out=plane[32 * quad : 32 * quad + 4, :].bitcast(I32),
-                                  in_=rows[0, 4 * quad : 4 * quad + 4, :].bitcast(I32))
+        def load_scales(queue, plane, rows, quads):
+            for quad in quads:
+                queue.dma_start(out=plane[32 * quad : 32 * quad + 4, :].bitcast(I32),
+                                in_=rows[0, 4 * quad : 4 * quad + 4, :].bitcast(I32))
 
         q_raw = sb.tile([P, PACK, Q], F32)
         key_words = sb.tile([P, 2 * T], U8, align_bytes=64)
         note_words = sb.tile([P, U], U32, align_bytes=64, tag="notes_then_third")
         nc.sync.dma_start(out=q_raw[:], in_=query.rearrange("(p j) q -> p j q", j=PACK))
-        load_scales(key_scale, keys_scales)
+        load_scales(nc.sync, key_scale, keys_scales, range(4))
         nc.sync.dma_start(out=key_words[:].bitcast(I32), in_=keys_words[0].bitcast(I32))
         nc.sync.dma_start(out=note_words[:].bitcast(I32),
                           in_=notes_words[0].rearrange("p u t -> p (u t)").bitcast(I32))
-        load_scales(note_scale, notes_scales)
+        load_scales(nc.sync, note_scale, notes_scales, [0, 1])
+        load_scales(nc.gpsimd, note_scale, notes_scales, [2, 3])
         nc.sync.dma_start(l_a1[:], offs)
         nc.sync.dma_start(l_a3[:], offs3)
         nc.sync.dma_start(l_b2[:], offs2)
         nc.sync.dma_start(l_put[:], offs4)
         nc.sync.dma_start(l_bb[:], offs5)
 
-        q_bf = sb.tile([P, Q, PACK], BF16, align_bytes=64)
-        nc.vector.tensor_copy(out=q_bf[:], in_=q_raw[:].rearrange("p j q -> p q j"))
+        q_bf = sb.tile([P, Q, PACK], BF16, align_bytes=64, tag="query_then_gaps")
+        q_turned = q_raw[:].rearrange("p j q -> p q j")
+        nc.vector.tensor_copy(out=q_bf[:, 0:Q_VECTOR, :], in_=q_turned[:, 0:Q_VECTOR, :])
+        nc.scalar.activation(q_bf[:, Q_VECTOR:Q, :], q_turned[:, Q_VECTOR:Q, :], COPY)
         q_words = sb.tile([P, Q], U32, align_bytes=64)
         q_scale = sb.tile([P, Q], U8, align_bytes=64)
         nc.vector.quantize_mx(out=q_words[:].bitcast(FP8X4), scales=q_scale[:],
                               in_=q_bf[:].rearrange("p q j -> p (q j)"))
+
+        gaps = sb.tile([P, U], F32, align_bytes=64, tag="query_then_gaps")
+        nc.vector.memset(gaps[:], 0.0)
 
         def score(name, rhs, rhs_scale, width):
             bank = ps.tile([P, width], F32, name=name)
@@ -92,35 +98,46 @@ def tile_attend_clippedgap_two_kernel(tc, query, keys_words, keys_scales, notes_
                 nc.scalar.activation(a[:, c0 : c0 + w], bank[:], COPY)
             else:
                 nc.vector.tensor_copy(a[:, c0 : c0 + w], bank[:])
-        first = sb.tile([P, HALF], F32, name="first0", tag="first")
-        nc.vector.tensor_copy(first[:], a[:].indirect(half(l_a1, 0)))
-        for n, (c0, w, bank) in enumerate(b_banks):
-            if n < 3:
-                nc.scalar.activation(b[:, c0 : c0 + w], bank[:], COPY)
-            else:
-                nc.vector.tensor_copy(b[:, c0 : c0 + w], bank[:])
-        neg_note = [sb.tile([P, HALF], F32, name="neg_note%d" % h) for h in range(2)]
-        for h in range(2):
-            nc.scalar.activation(neg_note[h][:], b[:].indirect(half(l_b2, h)), COPY, scale=-1.0)
-        third = sb.tile([P, HALF], F32, name="third0", align_bytes=64, tag="notes_then_third")
-        nc.vector.tensor_copy(third[:], a[:].indirect(half(l_a3, 0)))
+        first = sb.tile([P, SLOTS], F32)
+        nc.vector.tensor_copy(first[:], a[:].indirect(l_a1[:]))
+        for c0, w, bank in b_banks:
+            nc.scalar.activation(b[:, c0 : c0 + w], bank[:], COPY)
 
+        neg_note = [sb.tile([P, HALF], F32, name="neg_note%d" % h) for h in range(2)]
         neg_lo = [sb.tile([P, HALF], F32, name="neg_lo%d" % h) for h in range(2)]
         hi = [sb.tile([P, HALF], F32, name="hi%d" % h) for h in range(2)]
-        for h in range(2):
-            if h == 1:
-                first = sb.tile([P, HALF], F32, name="first1", tag="first")
-                nc.scalar.activation(first[:], a[:].indirect(half(l_a1, 1)), COPY)
-                third = sb.tile([P, HALF], F32, name="third1", align_bytes=64, tag="notes_then_third")
-                nc.scalar.activation(third[:], a[:].indirect(half(l_a3, 1)), COPY)
-            nc.vector.scalar_tensor_tensor(out=neg_lo[h][:], in0=first[:], scalar=-1.0, in1=neg_note[h][:],
-                                           op0=ALU.mult, op1=ALU.max)
+
+        def pick_third(h):
+            third = sb.tile([P, HALF], F32, name="third%d" % h, align_bytes=64, tag="notes_then_third")
+            nc.scalar.activation(third[:], a[:].indirect(half(l_a3, h)), COPY)
+            return third
+
+        def lower(h):
+            nc.vector.scalar_tensor_tensor(out=neg_lo[h][:], in0=first[:, h * HALF : (h + 1) * HALF], scalar=-1.0,
+                                           in1=neg_note[h][:], op0=ALU.mult, op1=ALU.max)
+
+        def upper(h, third):
             nc.vector.scalar_tensor_tensor(out=hi[h][:], in0=neg_note[h][:], scalar=-1.0, in1=third[:],
                                            op0=ALU.mult, op1=ALU.max)
+
+        def put_gaps(h):
             nc.vector.tensor_tensor(gaps[:].indirect(half(l_put, h)), hi[h][:], neg_lo[h][:], ALU.add)
 
+        third0 = pick_third(0)
+        nc.vector.tensor_scalar(neg_note[0][:], b[:].indirect(half(l_b2, 0)), -1.0, 0.0, ALU.mult, ALU.add)
+        nc.scalar.activation(neg_note[1][:], b[:].indirect(half(l_b2, 1)), COPY, scale=-1.0)
+        lower(0)
+        upper(0, third0)
+        third1 = pick_third(1)
+        lower(1)
+        put_gaps(0)
+        upper(1, third1)
+        put_gaps(1)
+
         bb = sb.tile([P, U], F32)
-        nc.vector.tensor_tensor(bb[:], b[:], gaps[:], ALU.subtract)
+        for c0, w, bank in b_banks[:3]:
+            nc.vector.tensor_tensor(bb[:, c0 : c0 + w], bank[:, 0:w], gaps[:, c0 : c0 + w], ALU.subtract)
+        nc.gpsimd.tensor_tensor(bb[:, BB_VECTOR:U], b[:, BB_VECTOR:U], gaps[:, BB_VECTOR:U], ALU.subtract)
 
         res0 = sb.tile([P, HALF], F32)
         nc.vector.tensor_tensor(res0[:], bb[:].indirect(half(l_bb, 0)), neg_lo[0][:], ALU.subtract)
@@ -129,4 +146,4 @@ def tile_attend_clippedgap_two_kernel(tc, query, keys_words, keys_scales, notes_
         nc.scalar.activation(left1[:], bb[:].indirect(half(l_bb, 1)), COPY)
         res1 = sb.tile([P, HALF], F32)
         nc.vector.tensor_tensor(res1[:], left1[:], neg_lo[1][:], ALU.subtract)
-        nc.scalar.dma_start(out=out[:, HALF:SLOTS], in_=res1[:])
+        nc.sync.dma_start(out=out[:, HALF:SLOTS], in_=res1[:])

@@ -95,9 +95,9 @@ def tile_attend_clippedgap_two_kernel(tc, query, keys_words, keys_scales, notes_
 
         for n, (c0, w, bank) in enumerate(a_banks):
             if n == 0:
-                nc.scalar.activation(a[:, c0 : c0 + w], bank[:], COPY)
-            else:
                 nc.vector.tensor_copy(a[:, c0 : c0 + w], bank[:])
+            else:
+                nc.scalar.activation(a[:, c0 : c0 + w], bank[:], COPY)
         first = sb.tile([P, SLOTS], F32)
         nc.vector.tensor_copy(first[:], a[:].indirect(l_a1[:]))
         for c0, w, bank in b_banks:

from contextlib import ExitStack

import concourse.mybir as mybir

D, T, U, SLOTS, Q = 512, 1024, 1024, 512, 128
FLOPS = 2 * D * Q * (T + U)

F32 = mybir.dt.float32
BF16 = mybir.dt.bfloat16
I32 = mybir.dt.int32
U32 = mybir.dt.uint32
U16 = mybir.dt.uint16
U8 = mybir.dt.uint8
FP8X4 = mybir.dt.float8_e4m3fn_x4
FP4X4 = mybir.dt.float4_e2m1fn_x4
ALU = mybir.AluOpType
COPY = mybir.ActivationFunctionType.Copy

P = 128
PACK = 4
HALF = SLOTS // 2
HALF_COLS = HALF // 16
Q_VECTOR = 88
BB_VECTOR = 768


def tile_attend_clippedgap_two_kernel(tc, query, keys_words, keys_scales, notes_words, notes_scales,
                                       offs, offs2, offs3, offs4, offs5, out):
    nc = tc.nc
    with ExitStack() as ctx:
        sb = ctx.enter_context(tc.tile_pool(name="sb", bufs=1))
        ps = ctx.enter_context(tc.psum_pool(name="ps", bufs=1))

        lists = [sb.tile([P, SLOTS // 16], U16, name="list%d" % n) for n in range(5)]
        l_a1, l_b2, l_a3, l_put, l_bb = lists

        key_scale = sb.tile([P, T], U8, align_bytes=64)
        note_scale = sb.tile([P, U], U8, align_bytes=64)

        def load_scales(queue, plane, rows, quads):
            for quad in quads:
                queue.dma_start(out=plane[32 * quad : 32 * quad + 4, :].bitcast(I32),
                                in_=rows[0, 4 * quad : 4 * quad + 4, :].bitcast(I32))

        q_raw = sb.tile([P, PACK, Q], F32)
        key_words = sb.tile([P, 2 * T], U8, align_bytes=64)
        note_words = sb.tile([P, U], U32, align_bytes=64, tag="notes_then_third")
        nc.sync.dma_start(out=q_raw[:], in_=query.rearrange("(p j) q -> p j q", j=PACK))
        load_scales(nc.sync, key_scale, keys_scales, range(4))
        nc.sync.dma_start(out=key_words[:].bitcast(I32), in_=keys_words[0].bitcast(I32))
        nc.sync.dma_start(out=note_words[:].bitcast(I32),
                          in_=notes_words[0].rearrange("p u t -> p (u t)").bitcast(I32))
        load_scales(nc.sync, note_scale, notes_scales, [0, 1])
        load_scales(nc.gpsimd, note_scale, notes_scales, [2, 3])
        nc.sync.dma_start(l_a1[:], offs)
        nc.sync.dma_start(l_a3[:], offs3)
        nc.sync.dma_start(l_b2[:], offs2)
        nc.sync.dma_start(l_put[:], offs4)
        nc.sync.dma_start(l_bb[:], offs5)

        q_bf = sb.tile([P, Q, PACK], BF16, align_bytes=64, tag="query_then_gaps")
        q_turned = q_raw[:].rearrange("p j q -> p q j")
        nc.vector.tensor_copy(out=q_bf[:, 0:Q_VECTOR, :], in_=q_turned[:, 0:Q_VECTOR, :])
        nc.scalar.activation(q_bf[:, Q_VECTOR:Q, :], q_turned[:, Q_VECTOR:Q, :], COPY)
        q_words = sb.tile([P, Q], U32, align_bytes=64)
        q_scale = sb.tile([P, Q], U8, align_bytes=64)
        nc.vector.quantize_mx(out=q_words[:].bitcast(FP8X4), scales=q_scale[:],
                              in_=q_bf[:].rearrange("p q j -> p (q j)"))

        gaps = sb.tile([P, U], F32, align_bytes=64, tag="query_then_gaps")
        nc.vector.memset(gaps[:], 0.0)

        def score(name, rhs, rhs_scale, width):
            bank = ps.tile([P, width], F32, name=name)
            nc.tensor.matmul_mx(out=bank[:], lhsT=q_words[:].bitcast(FP8X4), lhsT_scale=q_scale[:],
                                rhs=rhs, rhs_scale=rhs_scale, start=True, stop=True)
            return bank

        def key_score(c0, width):
            return score("a%d" % c0, key_words[:, 2 * c0 : 2 * (c0 + width)].bitcast(FP4X4),
                         key_scale[:, c0 : c0 + width], width)

        def note_score(c0, width):
            return score("b%d" % c0, note_words[:, c0 : c0 + width].bitcast(FP8X4),
                         note_scale[:, c0 : c0 + width], width)

        a = sb.tile([P, T], F32)
        b = sb.tile([P, U], F32)

        def half(lst, h):
            return lst[:, h * HALF_COLS : (h + 1) * HALF_COLS]

        a_banks = [(c0, w, key_score(c0, w)) for c0, w in ((0, 512), (512, 256), (768, 256))]
        b_banks = [(c0, 256, note_score(c0, 256)) for c0 in range(0, U, 256)]

        for n, (c0, w, bank) in enumerate(a_banks):
            if n == 0:
                nc.vector.tensor_copy(a[:, c0 : c0 + w], bank[:])
            else:
                nc.scalar.activation(a[:, c0 : c0 + w], bank[:], COPY)
        first = sb.tile([P, SLOTS], F32)
        nc.vector.tensor_copy(first[:], a[:].indirect(l_a1[:]))
        for c0, w, bank in b_banks:
            nc.scalar.activation(b[:, c0 : c0 + w], bank[:], COPY)

        neg_note = [sb.tile([P, HALF], F32, name="neg_note%d" % h) for h in range(2)]
        neg_lo = [sb.tile([P, HALF], F32, name="neg_lo%d" % h) for h in range(2)]
        hi = [sb.tile([P, HALF], F32, name="hi%d" % h) for h in range(2)]

        def pick_third(h):
            third = sb.tile([P, HALF], F32, name="third%d" % h, align_bytes=64, tag="notes_then_third")
            nc.scalar.activation(third[:], a[:].indirect(half(l_a3, h)), COPY)
            return third

        def lower(h):
            nc.vector.scalar_tensor_tensor(out=neg_lo[h][:], in0=first[:, h * HALF : (h + 1) * HALF], scalar=-1.0,
                                           in1=neg_note[h][:], op0=ALU.mult, op1=ALU.max)

        def upper(h, third):
            nc.vector.scalar_tensor_tensor(out=hi[h][:], in0=neg_note[h][:], scalar=-1.0, in1=third[:],
                                           op0=ALU.mult, op1=ALU.max)

        def put_gaps(h):
            nc.vector.tensor_tensor(gaps[:].indirect(half(l_put, h)), hi[h][:], neg_lo[h][:], ALU.add)

        third0 = pick_third(0)
        nc.vector.tensor_scalar(neg_note[0][:], b[:].indirect(half(l_b2, 0)), -1.0, 0.0, ALU.mult, ALU.add)
        nc.scalar.activation(neg_note[1][:], b[:].indirect(half(l_b2, 1)), COPY, scale=-1.0)
        lower(0)
        upper(0, third0)
        third1 = pick_third(1)
        lower(1)
        put_gaps(0)
        upper(1, third1)
        put_gaps(1)

        bb = sb.tile([P, U], F32)
        for c0, w, bank in b_banks[:3]:
            nc.vector.tensor_tensor(bb[:, c0 : c0 + w], bank[:, 0:w], gaps[:, c0 : c0 + w], ALU.subtract)
        nc.gpsimd.tensor_tensor(bb[:, BB_VECTOR:U], b[:, BB_VECTOR:U], gaps[:, BB_VECTOR:U], ALU.subtract)

        res0 = sb.tile([P, HALF], F32)
        nc.vector.tensor_tensor(res0[:], bb[:].indirect(half(l_bb, 0)), neg_lo[0][:], ALU.subtract)
        nc.sync.dma_start(out=out[:, 0:HALF], in_=res0[:])
        left1 = sb.tile([P, HALF], F32)
        nc.scalar.activation(left1[:], bb[:].indirect(half(l_bb, 1)), COPY)
        res1 = sb.tile([P, HALF], F32)
        nc.vector.tensor_tensor(res1[:], left1[:], neg_lo[1][:], ALU.subtract)
        nc.sync.dma_start(out=out[:, HALF:SLOTS], in_=res1[:])
